import numpy as np
import ml_dtypes


def mxq(x, axis, fmt="e4m3"):
    dtype, down = {"e4m3": (ml_dtypes.float8_e4m3fn, 7), "e5m2": (ml_dtypes.float8_e5m2, 14)}[fmt]
    v = np.moveaxis(np.asarray(x, np.float32).astype(ml_dtypes.bfloat16).astype(np.float64), axis, -1)
    blocks = v.reshape(v.shape[:-1] + (-1, 32))
    amax = np.abs(blocks).max(-1, keepdims=True)
    byte = np.maximum(np.where(amax > 0, np.frexp(amax)[1] - 1 + 127, 0) - down, 1)
    scale = np.exp2(byte - 127.0)
    codes = (blocks / scale).astype(np.float32).astype(dtype).astype(np.float64)
    return np.moveaxis((codes * scale).reshape(v.shape), -1, axis)


WIDE = False


def mx_kscale(k):
    if not WIDE:
        return np.ones(k)
    levels = np.array([10, -10, 5, -5, 0])
    if k % 512:
        return np.exp2(np.random.permutation(np.resize(levels, k // 32))).repeat(32)
    a = np.empty((k // 512, 16))
    for p in range(k // 512):
        a[p, :8] = np.random.permutation(np.resize(levels, 8))
        for g in range(8):
            far = levels[np.abs(levels - a[p, g]) >= 10]
            a[p, g + 8] = far[np.random.randint(len(far))]
    return np.exp2(a.ravel()).repeat(32)


def f64(x):
    return np.asarray(x).astype(np.float64)


def striped(idx):
    return np.tile(idx.reshape(-1, 16).T, (8, 1)).astype(np.uint16)


def unstriped(offs):
    return offs[:16].T.reshape(-1).astype(np.int64)


def striped8(idx):
    return np.concatenate([x.reshape(-1, 16).T for x in idx]).astype(np.uint16)


def runs(offs, k):
    lists = np.stack([offs[16 * r : 16 * r + 16].T.reshape(-1) for r in range(8)]).astype(np.int64)
    return lists[np.arange(k) % 512 // 64]


def pack_weight(w):
    k, n = w.shape
    w = f64(np.asarray(w, np.float32).astype(ml_dtypes.bfloat16)).reshape(k // 32, 32, n)
    amax = np.abs(w).max(1)
    byte = np.clip(np.where(amax > 0, np.frexp(amax)[1] - 1 + 127 - 7, 1), 1, 254)
    scaled = (w * np.exp2(127.0 - byte)[:, None, :]).reshape(k, n).astype(np.float32)
    words = np.ascontiguousarray(scaled.reshape(k // 512, 128, 4, n).transpose(0, 1, 3, 2)).astype(ml_dtypes.float8_e4m3fn).view(np.uint8)
    return words, np.ascontiguousarray(byte.astype(np.uint8).reshape(k // 512, 16, n))


def unpack_weight(words, scales):
    g, p, n, _ = words.shape
    vals = np.ascontiguousarray(words).view(ml_dtypes.float8_e4m3fn).astype(np.float64) * np.repeat(np.exp2(scales.astype(np.float64) - 127.0), 8, axis=1)[..., None]
    return vals.transpose(0, 1, 3, 2).reshape(g * 512, n)


def sigmoid(v):
    return 1.0 / (1.0 + np.exp(-np.maximum(v, -700.0)))


K, T, S, H, G, J = 512, 2048, 512, 512, 2048, 512


def setup_inputs():
    n = np.random.standard_normal
    s = mx_kscale(K)[:, None]
    packed_xT = pack_weight(n((K, T)) * s)
    packed_dT = pack_weight(n((K, G)) / s)
    return {
        "x_words": packed_xT[0],
        "x_scales": packed_xT[1],
        "w1": (n((K, H)) / np.sqrt(K) / s).astype(np.float32),
        "gs": (np.random.uniform(0.5, 1.5, (K, 1)) * s).astype(np.float32),
        "d_words": packed_dT[0],
        "d_scales": packed_dT[1],
        "tab": n((H, J)).astype(np.float32),
        "offs": striped(np.random.permutation(T)[:S]),
        "n1": striped8(np.stack([np.random.permutation(S) for _ in range(8)])),
        "n2": striped8(np.stack([np.random.permutation(S) for _ in range(8)])),
        "n3": striped8(np.stack([np.random.permutation(S) for _ in range(8)])),
        "k1": striped8(np.random.randint(0, G, (8, H))),
        "n4": striped8(np.random.randint(0, J, (8, S))),
        "n5": striped8(np.random.randint(0, J, (8, S))),
        "n6": striped8(np.stack([np.random.permutation(S) for _ in range(8)])),
    }


def reference(x_words, x_scales, w1, gs, d_words, d_scales, tab, offs, n1, n2, n3, k1, n4, n5, n6):
    d_k1 = unpack_weight(d_words, d_scales)[np.arange(K)[:, None], runs(k1, K)]
    xq = unpack_weight(x_words, x_scales)[:, unstriped(offs)]
    y = mxq(f64(w1), 0, "e4m3").T @ xq
    z = f64(gs) * ((y[np.arange(H)[:, None], runs(n1, H)]) * sigmoid(y) + (y[np.arange(H)[:, None], runs(n2, H)]) * (sigmoid(y[np.arange(H)[:, None], runs(n3, H)])))
    h = 0.0625 * ((d_k1.T @ mxq(z, 0, "e4m3")))
    return (h[np.arange(H)[:, None], runs(n6, H)]) * (f64(tab)[np.arange(H)[:, None], runs(n4, H)]) + f64(tab)[np.arange(H)[:, None], runs(n5, H)]

@@ -1,0 +1,245 @@
+from contextlib import ExitStack
+
+import concourse.mybir as mybir
+from concourse.masks import make_identity
+
+K, T, S, H, G, J = 512, 2048, 512, 512, 2048, 512
+FLOPS = 2 * 2 * 512 * 512 * 512
+
+F32 = mybir.dt.float32
+BF16 = mybir.dt.bfloat16
+I32 = mybir.dt.int32
+U32 = mybir.dt.uint32
+U16 = mybir.dt.uint16
+U8 = mybir.dt.uint8
+FP8X4 = mybir.dt.float8_e4m3fn_x4
+MULT = mybir.AluOpType.mult
+ADD = mybir.AluOpType.add
+COPY = mybir.ActivationFunctionType.Copy
+SIGMOID = mybir.ActivationFunctionType.Sigmoid
+
+P = 128
+PACK = 4
+WIN = 2 * S
+HALF = S // 2
+
+
+def tile_picked_densewsumkinda_none_p_kernel(
+    tc, x_words, x_scales, w1, gs, d_words, d_scales, tab, offs, n1, n2, n3, k1, n4, n5, n6, out
+):
+    nc = tc.nc
+    with ExitStack() as ctx:
+        lists = ctx.enter_context(tc.tile_pool(name="lists", bufs=1))
+        sb = ctx.enter_context(tc.tile_pool(name="sb", bufs=1))
+        psum = ctx.enter_context(tc.psum_pool(name="psum", bufs=1))
+
+        def load_list(src, name):
+            tile = lists.tile([P, S // 16], U16, name=name)
+            nc.sync.dma_start(tile[:], src)
+            return tile
+
+        tab_rows = tab.rearrange("(p t) j -> p t j", t=PACK)
+        out_rows = out.rearrange("(p t) j -> p t j", t=PACK)
+        tab_win = [sb.tile([P, WIN], F32, name="tab_win%d" % t) for t in range(PACK)]
+
+        def load_tab(t):
+            nc.sync.dma_start(tab_win[t][:, 0:J], tab_rows[:, t, :])
+
+        xs_win = sb.tile([P, T], U8, name="xs_win", align_bytes=64)
+        ds_win = sb.tile([P, G], U8, name="ds_win")
+        d_plane = sb.tile([P, H], U8, name="d_plane", align_bytes=64)
+        nc.gpsimd.memset(xs_win[:].bitcast(I32), 0)
+        xs_rows = x_scales[0].rearrange("(q r) c -> r q c", r=4)
+        for r in range(4):
+            nc.gpsimd.dma_start(xs_win[r:P:32, :].bitcast(I32), xs_rows[r].bitcast(I32))
+        nc.vector.memset(ds_win[:].bitcast(I32), 0)
+        nc.vector.memset(d_plane[:].bitcast(I32), 0)
+        ds_rows = d_scales[0].rearrange("(g e) c -> e g c", e=2)
+        for e in range(2):
+            nc.gpsimd.dma_start(ds_win[e:P:16, :].bitcast(I32), ds_rows[e].bitcast(I32))
+        warm = sb.tile([P, 8], F32, name="warm")
+        nc.vector.memset(warm[:, 0:1], 0.0)
+        nc.scalar.activation(warm[:, 4:5], warm[:, 0:1], SIGMOID)
+
+        ident = sb.tile([P, P], F32, name="ident")
+        make_identity(nc, ident[:])
+
+        load_tab(0)
+        n4_t = load_list(n4, "n4_t")
+        load_tab(1)
+        offs_t = load_list(offs, "offs_t")
+        w_rows = w1.rearrange("(p j) c -> p j c", j=PACK)
+        w_raw = [sb.tile([P, PACK, H // 2], F32, name="w_raw%d" % i) for i in range(2)]
+        for i in range(2):
+            nc.sync.dma_start(w_raw[i][:], w_rows[:, :, i * H // 2 : (i + 1) * H // 2])
+        xw_win = sb.tile([P, T], U32, name="xw_win", align_bytes=64)
+        nc.sync.dma_start(xw_win[:].bitcast(I32), x_words[0].rearrange("p n t -> p (n t)").bitcast(I32))
+        k1_t = load_list(k1, "k1_t")
+        gs_t = sb.tile([P, PACK], F32, name="gs_t")
+        nc.sync.dma_start(gs_t[:], gs.rearrange("(p t) o -> p (t o)", t=PACK))
+        n1_t = load_list(n1, "n1_t")
+        n3_t = load_list(n3, "n3_t")
+        n2_t = load_list(n2, "n2_t")
+        dw_win = sb.tile([P, G], U32, name="dw_win")
+        nc.sync.dma_start(dw_win[:].bitcast(I32), d_words[0].rearrange("p n t -> p (n t)").bitcast(I32))
+        load_tab(2)
+        load_tab(3)
+        n6_t = load_list(n6, "n6_t")
+        n5_t = load_list(n5, "n5_t")
+
+        t4 = {}
+
+        def gather_t4(t, tag):
+            t4[t] = sb.tile([P, S], F32, name="t4_%d" % t, tag=tag, align_bytes=64)
+            nc.vector.tensor_copy(t4[t][:], tab_win[t][:].indirect(n4_t[:]))
+
+        gather_t4(0, "t4_0")
+        gather_t4(1, "t4_1")
+        x_plane = sb.tile([P, S], U8, name="x_plane", align_bytes=64)
+        nc.vector.tensor_copy(x_plane[:], xs_win[:].indirect(offs_t[:]))
+
+        w_bf = sb.tile([P, PACK, P, PACK], BF16, name="w_bf", align_bytes=64)
+        for i in range(2):
+            nc.scalar.copy(
+                w_bf[:, :, i * P // 2 : (i + 1) * P // 2, :].rearrange("p t m j -> p m t j"),
+                w_raw[i][:].rearrange("p j (m t) -> p m t j", t=PACK),
+            )
+        w_codes = sb.tile([P, H], U32, name="w_codes", tag="xs_win", align_bytes=64)
+        w_plane = sb.tile([P, H], U8, name="w_plane", align_bytes=64)
+        nc.vector.quantize_mx(w_codes[:].bitcast(FP8X4), w_plane[:], w_bf[:].rearrange("p t m j -> p (t m j)"))
+        x_codes = sb.tile([P, S], U32, name="x_codes", tag="w_bf", align_bytes=64)
+        nc.vector.tensor_copy(x_codes[:], xw_win[:].indirect(offs_t[:]))
+
+        d_got_plane = sb.tile([P, H], U8, name="d_got_plane", tag="xw_win", align_bytes=64)
+        nc.vector.tensor_copy(d_got_plane[:], ds_win[:].indirect(k1_t[:]))
+        d_dealt_plane = sb.tile([P, H], U8, name="d_dealt_plane")
+        nc.vector.tensor_copy(
+            d_dealt_plane[:].rearrange("p (t c i) -> p c t i", t=PACK, i=4),
+            d_got_plane[:].rearrange("p (c i t) -> p c t i", t=PACK, i=4),
+        )
+        for r in range(4):
+            src = 16 * (r // 2) + r % 2
+            nc.sync.dma_start(d_plane[r:P:32, :].bitcast(I32), d_dealt_plane[src:P:32, :].bitcast(I32))
+
+        y_bank = [psum.tile([P, S], F32, name="y_bank%d" % t, tag="bank%d" % t) for t in range(PACK)]
+        for t in range(PACK):
+            cols = slice(t * P, (t + 1) * P)
+            nc.tensor.matmul_mx(
+                y_bank[t][:], lhsT=w_codes[:, cols].bitcast(FP8X4), lhsT_scale=w_plane[:, cols],
+                rhs=x_codes[:].bitcast(FP8X4), rhs_scale=x_plane[:], start=True, stop=True,
+            )
+
+        terms = []
+        for t in range(PACK):
+            y_win = sb.tile([P, WIN], F32, name="y_win%d" % t)
+            g_win = sb.tile([P, WIN], F32, name="g_win%d" % t, align_bytes=64)
+            gate3 = sb.tile([P, S], F32, name="gate3_%d" % t, align_bytes=64)
+            term1 = sb.tile([P, S], F32, name="term1_%d" % t)
+            term2 = sb.tile([P, S], F32, name="term2_%d" % t)
+            nc.scalar.copy(y_win[:, 0:S], y_bank[t][:])
+            nc.scalar.activation(y_win[:, S:WIN], y_bank[t][:], SIGMOID)
+            if t < PACK - 1:
+                nc.vector.tensor_scalar(g_win[:, 0:S], y_win[:, 0:S], gs_t[:, t : t + 1], None, MULT)
+            else:
+                nc.scalar.activation(g_win[:, 0:S], y_bank[t][:], COPY, scale=gs_t[:, t : t + 1])
+            nc.scalar.activation(gate3[:], y_win[:].indirect(n3_t[:]), SIGMOID)
+            nc.vector.tensor_tensor(term1[:], g_win[:].indirect(n1_t[:]), y_win[:, S:WIN], MULT)
+            pieces = 1 if t < PACK - 1 else 2
+            width = S // pieces
+            for i in range(pieces):
+                cols = slice(i * width, (i + 1) * width)
+                offsets = n2_t[:, i * width // 16 : (i + 1) * width // 16]
+                nc.vector.tensor_tensor(term2[:, cols], g_win[:].indirect(offsets), gate3[:, cols], MULT)
+            terms.append((term1, term2))
+
+        def add_turned(dst, t, which, b):
+            nc.tensor.matmul(
+                dst, lhsT=terms[t][which][:, b * P : (b + 1) * P], rhs=ident[:],
+                start=which == 0, stop=which == 1, is_transpose=True,
+            )
+
+        low = [psum.tile([P, 2, 2, P], F32, name="low%d" % hb, tag="bank%d" % (4 + hb)) for hb in range(2)]
+        for t in range(2):
+            for b in range(4):
+                for which in range(2):
+                    add_turned(low[b // 2][:, b % 2, t, :], t, which, b)
+        high = [psum.tile([P, 2, P], F32, name="high%d" % b, tag="bank%d" % ((6 + b) % 8)) for b in range(4)]
+        back = [psum.tile([P, 2, 2, P], F32, name="back%d" % hb, tag="bank%d" % (2 + hb)) for hb in range(2)]
+        for which in range(2):
+            for b in range(4):
+                add_turned(high[b][:, 0, :], 2, which, b)
+        for hb in range(2):
+            low_bf = sb.tile([P, 2, P, 2], BF16, name="low_bf%d" % hb)
+            nc.scalar.copy(low_bf[:], low[hb][:].rearrange("k b e p -> k b p e"))
+            for b in range(2):
+                nc.tensor.transpose(
+                    back[hb][:, b, 0, :], low_bf[:, b].rearrange("k p e -> k (p e)").bitcast(F32), ident[:]
+                )
+        for which in range(2):
+            for b in range(4):
+                add_turned(high[b][:, 1, :], 3, which, b)
+        z_bf = []
+        for hb in range(2):
+            for b in range(2 * hb, 2 * hb + 2):
+                high_bf = sb.tile([P, P, 2], BF16, name="high_bf%d" % b)
+                nc.scalar.copy(high_bf[:], high[b][:].rearrange("k e p -> k p e"))
+                nc.tensor.transpose(
+                    back[hb][:, b % 2, 1, :], high_bf[:].rearrange("k p e -> k (p e)").bitcast(F32), ident[:]
+                )
+            z_bf.append(sb.tile([P, HALF, PACK], BF16, name="z_bf%d" % hb, align_bytes=64))
+            z_words = z_bf[hb][:].rearrange("p k t -> p (k t)").bitcast(F32)
+            nc.scalar.copy(
+                z_words.rearrange("p (b k u) -> p b k u", b=2, u=2), back[hb][:].rearrange("p b u k -> p b k u")
+            )
+
+        d_got = sb.tile([P, H], U32, name="d_got", tag="gate3_3", align_bytes=64)
+        nc.vector.tensor_copy(d_got[:], dw_win[:].indirect(k1_t[:]))
+        d_codes = sb.tile([P, H], U32, name="d_codes", align_bytes=64)
+        nc.vector.tensor_copy(
+            d_codes[:].bitcast(I32).rearrange("p (t c i) -> p c t i", t=PACK, i=4),
+            d_got[:].bitcast(I32).rearrange("p (c i t) -> p c t i", t=PACK, i=4),
+        )
+        gather_t4(2, "gate3_3")
+        z_codes = sb.tile([P, S], U32, name="z_codes", align_bytes=64)
+        z_plane = sb.tile([P, S], U8, name="z_plane", align_bytes=64)
+        for hb in range(2):
+            half = slice(hb * HALF, (hb + 1) * HALF)
+            nc.vector.quantize_mx(
+                z_codes[:, half].bitcast(FP8X4), z_plane[:, half], z_bf[hb][:].rearrange("p k t -> p (k t)")
+            )
+        gather_t4(3, "z_bf1")
+
+        h_bank = [psum.tile([P, S], F32, name="h_bank%d" % t, tag="bank%d" % (4 + t)) for t in range(PACK)]
+        for t in range(PACK):
+            cols = slice(t * P, (t + 1) * P)
+            for hb in range(2):
+                half = slice(hb * HALF, (hb + 1) * HALF)
+                nc.tensor.matmul_mx(
+                    h_bank[t][:, half],
+                    lhsT=d_codes[:, cols].bitcast(FP8X4), lhsT_scale=d_plane[:, cols],
+                    rhs=z_codes[:, half].bitcast(FP8X4), rhs_scale=z_plane[:, half], start=True, stop=True,
+                )
+
+        prods = []
+
+        def product(t):
+            h_win = sb.tile([P, WIN], F32, name="h_win%d" % t)
+            nc.scalar.activation(h_win[:, 0:S], h_bank[t][:], COPY, scale=0.0625)
+            prod = sb.tile([P, S], F32, name="prod%d" % t)
+            nc.vector.tensor_tensor(prod[:], h_win[:].indirect(n6_t[:]), t4[t][:], MULT)
+            prods.append(prod)
+
+        def finish(t, pieces):
+            width = S // pieces
+            for i in range(pieces):
+                cols = slice(i * width, (i + 1) * width)
+                res = sb.tile([P, width], F32, name="res%d_%d" % (t, i))
+                offsets = n5_t[:, i * width // 16 : (i + 1) * width // 16]
+                nc.vector.tensor_tensor(res[:], tab_win[t][:].indirect(offsets), prods[t][:, cols], ADD)
+                nc.sync.dma_start(out_rows[:, t, cols], res[:])
+
+        product(0)
+        for t in range(1, PACK):
+            product(t)
+            finish(t - 1, 1)
+        finish(PACK - 1, 2)

@@ -40,50 +40,47 @@ def tile_picked_densewsumkinda_none_p_kernel(
 
         tab_rows = tab.rearrange("(p t) j -> p t j", t=PACK)
         out_rows = out.rearrange("(p t) j -> p t j", t=PACK)
-        tab_win = [sb.tile([P, WIN], F32, name="tab_win%d" % t) for t in range(PACK)]
+        tab_win = {}
 
-        def load_tab(t):
-            nc.sync.dma_start(tab_win[t][:, 0:J], tab_rows[:, t, :])
+        def load_tab(t, queue, tag):
+            tab_win[t] = sb.tile([P, WIN], F32, name="tab_win%d" % t, tag=tag, align_bytes=64)
+            queue.dma_start(tab_win[t][:, 0:J], tab_rows[:, t, :])
 
         xs_win = sb.tile([P, T], U8, name="xs_win", align_bytes=64)
-        ds_win = sb.tile([P, G], U8, name="ds_win")
+        ds_win = sb.tile([P, G], U8, name="ds_win", align_bytes=64)
         d_plane = sb.tile([P, H], U8, name="d_plane", align_bytes=64)
         nc.gpsimd.memset(xs_win[:].bitcast(I32), 0)
-        xs_rows = x_scales[0].rearrange("(q r) c -> r q c", r=4)
-        for r in range(4):
-            nc.gpsimd.dma_start(xs_win[r:P:32, :].bitcast(I32), xs_rows[r].bitcast(I32))
-        nc.vector.memset(ds_win[:].bitcast(I32), 0)
-        nc.vector.memset(d_plane[:].bitcast(I32), 0)
-        ds_rows = d_scales[0].rearrange("(g e) c -> e g c", e=2)
-        for e in range(2):
-            nc.gpsimd.dma_start(ds_win[e:P:16, :].bitcast(I32), ds_rows[e].bitcast(I32))
         warm = sb.tile([P, 8], F32, name="warm")
         nc.vector.memset(warm[:, 0:1], 0.0)
-        nc.scalar.activation(warm[:, 4:5], warm[:, 0:1], SIGMOID)
+        nc.vector.memset(ds_win[:].bitcast(I32), 0)
+        nc.vector.memset(d_plane[:].bitcast(I32), 0)
 
         ident = sb.tile([P, P], F32, name="ident")
         make_identity(nc, ident[:])
 
-        load_tab(0)
         n4_t = load_list(n4, "n4_t")
-        load_tab(1)
+        load_tab(0, nc.scalar, "tab_win0")
         offs_t = load_list(offs, "offs_t")
+        load_tab(1, nc.scalar, "tab_win1")
+        xs_rows = x_scales[0].rearrange("(q r) c -> r q c", r=4)
+        for r in range(4):
+            nc.sync.dma_start(xs_win[r:P:32, :].bitcast(I32), xs_rows[r].bitcast(I32))
         w_rows = w1.rearrange("(p j) c -> p j c", j=PACK)
-        w_raw = [sb.tile([P, PACK, H // 2], F32, name="w_raw%d" % i) for i in range(2)]
+        w_raw = [sb.tile([P, PACK, H // 2], F32, name="w_raw%d" % i, align_bytes=64) for i in range(2)]
         for i in range(2):
-            nc.sync.dma_start(w_raw[i][:], w_rows[:, :, i * H // 2 : (i + 1) * H // 2])
+            nc.scalar.dma_start(w_raw[i][:], w_rows[:, :, i * H // 2 : (i + 1) * H // 2])
         xw_win = sb.tile([P, T], U32, name="xw_win", align_bytes=64)
-        nc.sync.dma_start(xw_win[:].bitcast(I32), x_words[0].rearrange("p n t -> p (n t)").bitcast(I32))
+        nc.scalar.dma_start(xw_win[:].bitcast(I32), x_words[0].rearrange("p n t -> p (n t)").bitcast(I32))
+        nc.scalar.activation(warm[:, 4:5], warm[:, 0:1], SIGMOID)
         k1_t = load_list(k1, "k1_t")
+        ds_rows = d_scales[0].rearrange("(g e) c -> e g c", e=2)
+        for e in range(2):
+            nc.sync.dma_start(ds_win[e:P:16, :].bitcast(I32), ds_rows[e].bitcast(I32))
         gs_t = sb.tile([P, PACK], F32, name="gs_t")
         nc.sync.dma_start(gs_t[:], gs.rearrange("(p t) o -> p (t o)", t=PACK))
         n1_t = load_list(n1, "n1_t")
         n3_t = load_list(n3, "n3_t")
         n2_t = load_list(n2, "n2_t")
-        dw_win = sb.tile([P, G], U32, name="dw_win")
-        nc.sync.dma_start(dw_win[:].bitcast(I32), d_words[0].rearrange("p n t -> p (n t)").bitcast(I32))
-        load_tab(2)
-        load_tab(3)
         n6_t = load_list(n6, "n6_t")
         n5_t = load_list(n5, "n5_t")
 
@@ -104,6 +101,7 @@ def tile_picked_densewsumkinda_none_p_kernel(
                 w_bf[:, :, i * P // 2 : (i + 1) * P // 2, :].rearrange("p t m j -> p m t j"),
                 w_raw[i][:].rearrange("p j (m t) -> p m t j", t=PACK),
             )
+        load_tab(2, nc.sync, "w_raw1")
         w_codes = sb.tile([P, H], U32, name="w_codes", tag="xs_win", align_bytes=64)
         w_plane = sb.tile([P, H], U8, name="w_plane", align_bytes=64)
         nc.vector.quantize_mx(w_codes[:].bitcast(FP8X4), w_plane[:], w_bf[:].rearrange("p t m j -> p (t m j)"))
@@ -120,6 +118,9 @@ def tile_picked_densewsumkinda_none_p_kernel(
         for r in range(4):
             src = 16 * (r // 2) + r % 2
             nc.sync.dma_start(d_plane[r:P:32, :].bitcast(I32), d_dealt_plane[src:P:32, :].bitcast(I32))
+        dw_win = sb.tile([P, G], U32, name="dw_win", tag="ds_win", align_bytes=64)
+        nc.sync.dma_start(dw_win[:].bitcast(I32), d_words[0].rearrange("p n t -> p (n t)").bitcast(I32))
+        load_tab(3, nc.sync, "xw_win")
 
         y_bank = [psum.tile([P, S], F32, name="y_bank%d" % t, tag="bank%d" % t) for t in range(PACK)]
         for t in range(PACK):
@@ -136,12 +137,14 @@ def tile_picked_densewsumkinda_none_p_kernel(
             gate3 = sb.tile([P, S], F32, name="gate3_%d" % t, align_bytes=64)
             term1 = sb.tile([P, S], F32, name="term1_%d" % t)
             term2 = sb.tile([P, S], F32, name="term2_%d" % t)
-            nc.scalar.copy(y_win[:, 0:S], y_bank[t][:])
-            nc.scalar.activation(y_win[:, S:WIN], y_bank[t][:], SIGMOID)
-            if t < PACK - 1:
+            if t == 0:
+                nc.scalar.copy(y_win[:, 0:S], y_bank[t][:])
+                nc.scalar.activation(y_win[:, S:WIN], y_bank[t][:], SIGMOID)
                 nc.vector.tensor_scalar(g_win[:, 0:S], y_win[:, 0:S], gs_t[:, t : t + 1], None, MULT)
             else:
                 nc.scalar.activation(g_win[:, 0:S], y_bank[t][:], COPY, scale=gs_t[:, t : t + 1])
+                nc.scalar.activation(y_win[:, S:WIN], y_bank[t][:], SIGMOID)
+                nc.scalar.copy(y_win[:, 0:S], y_bank[t][:])
             nc.scalar.activation(gate3[:], y_win[:].indirect(n3_t[:]), SIGMOID)
             nc.vector.tensor_tensor(term1[:], g_win[:].indirect(n1_t[:]), y_win[:, S:WIN], MULT)
             pieces = 1 if t < PACK - 1 else 2
@@ -151,6 +154,8 @@ def tile_picked_densewsumkinda_none_p_kernel(
                 offsets = n2_t[:, i * width // 16 : (i + 1) * width // 16]
                 nc.vector.tensor_tensor(term2[:, cols], g_win[:].indirect(offsets), gate3[:, cols], MULT)
             terms.append((term1, term2))
+            if t == 0:
+                gather_t4(2, "gate3_0")
 
         def add_turned(dst, t, which, b):
             nc.tensor.matmul(
@@ -199,7 +204,6 @@ def tile_picked_densewsumkinda_none_p_kernel(
             d_codes[:].bitcast(I32).rearrange("p (t c i) -> p c t i", t=PACK, i=4),
             d_got[:].bitcast(I32).rearrange("p (c i t) -> p c t i", t=PACK, i=4),
         )
-        gather_t4(2, "gate3_3")
         z_codes = sb.tile([P, S], U32, name="z_codes", align_bytes=64)
         z_plane = sb.tile([P, S], U8, name="z_plane", align_bytes=64)
         for hb in range(2):

@@ -4,7 +4,7 @@ import concourse.mybir as mybir
 from concourse.masks import make_identity
 
 K, T, S, H, G, J = 512, 2048, 512, 512, 2048, 512
-FLOPS = 2 * 2 * 512 * 512 * 512
+FLOPS = 2 * K * H * S + 2 * H * H * S
 
 F32 = mybir.dt.float32
 BF16 = mybir.dt.bfloat16
@@ -19,9 +19,14 @@ COPY = mybir.ActivationFunctionType.Copy
 SIGMOID = mybir.ActivationFunctionType.Sigmoid
 
 P = 128
-PACK = 4
-WIN = 2 * S
+PLANES = 4
+LAST = PLANES - 1
+GROUP = 16
+QUAD = 32
+WINDOW = 2 * S
 HALF = S // 2
+BLOCKS = S // P
+ALIGN = 64
 
 
 def tile_picked_densewsumkinda_none_p_kernel(
@@ -34,145 +39,170 @@ def tile_picked_densewsumkinda_none_p_kernel(
         psum = ctx.enter_context(tc.psum_pool(name="psum", bufs=1))
 
         def load_list(src, name):
-            tile = lists.tile([P, S // 16], U16, name=name)
+            tile = lists.tile([P, S // GROUP], U16, name=name)
             nc.sync.dma_start(tile[:], src)
             return tile
 
-        tab_rows = tab.rearrange("(p t) j -> p t j", t=PACK)
-        out_rows = out.rearrange("(p t) j -> p t j", t=PACK)
+        tab_planes = tab.rearrange("(p t) j -> p t j", t=PLANES)
+        out_planes = out.rearrange("(p t) j -> p t j", t=PLANES)
         tab_win = {}
 
-        def load_tab(t, queue, tag):
-            tab_win[t] = sb.tile([P, WIN], F32, name="tab_win%d" % t, tag=tag, align_bytes=64)
-            queue.dma_start(tab_win[t][:, 0:J], tab_rows[:, t, :])
+        def load_tab(t, queue, slot):
+            tab_win[t] = sb.tile([P, WINDOW], F32, name="tab_win%d" % t, tag=slot, align_bytes=ALIGN)
+            queue.dma_start(tab_win[t][:, 0:J], tab_planes[:, t, :])
 
-        xs_win = sb.tile([P, T], U8, name="xs_win", align_bytes=64)
-        ds_win = sb.tile([P, G], U8, name="ds_win", align_bytes=64)
-        d_plane = sb.tile([P, H], U8, name="d_plane", align_bytes=64)
+        xs_win = sb.tile([P, T], U8, name="xs_win", align_bytes=ALIGN)
+        ds_win = sb.tile([P, G], U8, name="ds_win", align_bytes=ALIGN)
+        d_scale = sb.tile([P, H], U8, name="d_scale", align_bytes=ALIGN)
         nc.gpsimd.memset(xs_win[:].bitcast(I32), 0)
         warm = sb.tile([P, 8], F32, name="warm")
         nc.vector.memset(warm[:, 0:1], 0.0)
         nc.vector.memset(ds_win[:].bitcast(I32), 0)
-        nc.vector.memset(d_plane[:].bitcast(I32), 0)
+        nc.vector.memset(d_scale[:].bitcast(I32), 0)
 
         ident = sb.tile([P, P], F32, name="ident")
         make_identity(nc, ident[:])
 
         n4_t = load_list(n4, "n4_t")
+        n5_t = load_list(n5, "n5_t")
         load_tab(0, nc.scalar, "tab_win0")
         offs_t = load_list(offs, "offs_t")
         load_tab(1, nc.scalar, "tab_win1")
         xs_rows = x_scales[0].rearrange("(q r) c -> r q c", r=4)
         for r in range(4):
-            nc.sync.dma_start(xs_win[r:P:32, :].bitcast(I32), xs_rows[r].bitcast(I32))
-        w_rows = w1.rearrange("(p j) c -> p j c", j=PACK)
-        w_raw = [sb.tile([P, PACK, H // 2], F32, name="w_raw%d" % i, align_bytes=64) for i in range(2)]
+            nc.sync.dma_start(xs_win[r:P:QUAD, :].bitcast(I32), xs_rows[r].bitcast(I32))
+        w_rows = w1.rearrange("(p j) c -> p j c", j=PLANES)
+        w_raw = [sb.tile([P, PLANES, H // 2], F32, name="w_raw%d" % i, align_bytes=ALIGN) for i in range(2)]
         for i in range(2):
             nc.scalar.dma_start(w_raw[i][:], w_rows[:, :, i * H // 2 : (i + 1) * H // 2])
-        xw_win = sb.tile([P, T], U32, name="xw_win", align_bytes=64)
+        xw_win = sb.tile([P, T], U32, name="xw_win", align_bytes=ALIGN)
         nc.scalar.dma_start(xw_win[:].bitcast(I32), x_words[0].rearrange("p n t -> p (n t)").bitcast(I32))
         nc.scalar.activation(warm[:, 4:5], warm[:, 0:1], SIGMOID)
         k1_t = load_list(k1, "k1_t")
         ds_rows = d_scales[0].rearrange("(g e) c -> e g c", e=2)
         for e in range(2):
-            nc.sync.dma_start(ds_win[e:P:16, :].bitcast(I32), ds_rows[e].bitcast(I32))
-        gs_t = sb.tile([P, PACK], F32, name="gs_t")
-        nc.sync.dma_start(gs_t[:], gs.rearrange("(p t) o -> p (t o)", t=PACK))
+            nc.sync.dma_start(ds_win[e:P:GROUP, :].bitcast(I32), ds_rows[e].bitcast(I32))
+        gs_t = sb.tile([P, PLANES], F32, name="gs_t")
+        nc.sync.dma_start(gs_t[:], gs.rearrange("(p t) o -> p (t o)", t=PLANES))
         n1_t = load_list(n1, "n1_t")
         n3_t = load_list(n3, "n3_t")
         n2_t = load_list(n2, "n2_t")
         n6_t = load_list(n6, "n6_t")
-        n5_t = load_list(n5, "n5_t")
 
-        t4 = {}
+        tab_n4 = {}
 
-        def gather_t4(t, tag):
-            t4[t] = sb.tile([P, S], F32, name="t4_%d" % t, tag=tag, align_bytes=64)
-            nc.vector.tensor_copy(t4[t][:], tab_win[t][:].indirect(n4_t[:]))
+        def gather_tab_n4(t, slot):
+            tab_n4[t] = sb.tile([P, S], F32, name="tab_n4_%d" % t, tag=slot, align_bytes=ALIGN)
+            nc.vector.tensor_copy(tab_n4[t][:], tab_win[t][:].indirect(n4_t[:]))
 
-        gather_t4(0, "t4_0")
-        gather_t4(1, "t4_1")
-        x_plane = sb.tile([P, S], U8, name="x_plane", align_bytes=64)
-        nc.vector.tensor_copy(x_plane[:], xs_win[:].indirect(offs_t[:]))
+        gather_tab_n4(0, "tab_n4_0")
+        gather_tab_n4(1, "tab_n4_1")
+        tab_n5_first = sb.tile([P, S], F32, name="tab_n5_first")
+        nc.vector.tensor_copy(tab_n5_first[:], tab_win[0][:].indirect(n5_t[:]))
+        x_scale = sb.tile([P, S], U8, name="x_scale", align_bytes=ALIGN)
+        nc.vector.tensor_copy(x_scale[:], xs_win[:].indirect(offs_t[:]))
 
-        w_bf = sb.tile([P, PACK, P, PACK], BF16, name="w_bf", align_bytes=64)
-        for i in range(2):
+        w_bf = sb.tile([P, PLANES, P, PLANES], BF16, name="w_bf", align_bytes=ALIGN)
+        for i, planes in ((0, slice(0, 4)), (1, slice(0, 2)), (1, slice(2, 4))):
             nc.scalar.copy(
-                w_bf[:, :, i * P // 2 : (i + 1) * P // 2, :].rearrange("p t m j -> p m t j"),
-                w_raw[i][:].rearrange("p j (m t) -> p m t j", t=PACK),
+                w_bf[:, planes, i * P // 2 : (i + 1) * P // 2, :].rearrange("p t m j -> p m t j"),
+                w_raw[i][:].rearrange("p j (m t) -> p m t j", t=PLANES)[:, :, planes, :],
             )
-        load_tab(2, nc.sync, "w_raw1")
-        w_codes = sb.tile([P, H], U32, name="w_codes", tag="xs_win", align_bytes=64)
-        w_plane = sb.tile([P, H], U8, name="w_plane", align_bytes=64)
-        nc.vector.quantize_mx(w_codes[:].bitcast(FP8X4), w_plane[:], w_bf[:].rearrange("p t m j -> p (t m j)"))
-        x_codes = sb.tile([P, S], U32, name="x_codes", tag="w_bf", align_bytes=64)
+        w_codes = sb.tile([P, H], U32, name="w_codes", tag="xs_win", align_bytes=ALIGN)
+        w_scale = sb.tile([P, H], U8, name="w_scale", align_bytes=ALIGN)
+        x_codes = sb.tile([P, S], U32, name="x_codes", align_bytes=ALIGN)
+
+        def quantise_w(pair):
+            cols = slice(pair * H // 2, (pair + 1) * H // 2)
+            nc.vector.quantize_mx(
+                w_codes[:, cols].bitcast(FP8X4),
+                w_scale[:, cols],
+                w_bf[:, 2 * pair : 2 * pair + 2].rearrange("p t m j -> p (t m j)"),
+            )
+
+        quantise_w(0)
         nc.vector.tensor_copy(x_codes[:], xw_win[:].indirect(offs_t[:]))
+        quantise_w(1)
+        load_tab(2, nc.sync, "xw_win")
 
-        d_got_plane = sb.tile([P, H], U8, name="d_got_plane", tag="xw_win", align_bytes=64)
-        nc.vector.tensor_copy(d_got_plane[:], ds_win[:].indirect(k1_t[:]))
-        d_dealt_plane = sb.tile([P, H], U8, name="d_dealt_plane")
-        nc.vector.tensor_copy(
-            d_dealt_plane[:].rearrange("p (t c i) -> p c t i", t=PACK, i=4),
-            d_got_plane[:].rearrange("p (c i t) -> p c t i", t=PACK, i=4),
-        )
+        def deal_columns(dst, src):
+            nc.vector.tensor_copy(
+                dst.rearrange("p (t c i) -> p c t i", t=PLANES, i=4),
+                src.rearrange("p (c i t) -> p c t i", t=PLANES, i=4),
+            )
+
+        ds_got = sb.tile([P, H], U8, name="ds_got", tag="w_bf", align_bytes=ALIGN)
+        nc.vector.tensor_copy(ds_got[:], ds_win[:].indirect(k1_t[:]))
+        ds_dealt = sb.tile([P, H], U8, name="ds_dealt", align_bytes=ALIGN)
+        deal_columns(ds_dealt[:], ds_got[:])
         for r in range(4):
-            src = 16 * (r // 2) + r % 2
-            nc.sync.dma_start(d_plane[r:P:32, :].bitcast(I32), d_dealt_plane[src:P:32, :].bitcast(I32))
-        dw_win = sb.tile([P, G], U32, name="dw_win", tag="ds_win", align_bytes=64)
+            first = GROUP * (r // 2) + r % 2
+            nc.sync.dma_start(d_scale[r:P:QUAD, :].bitcast(I32), ds_dealt[first:P:QUAD, :].bitcast(I32))
+        dw_win = sb.tile([P, G], U32, name="dw_win", tag="ds_win", align_bytes=ALIGN)
         nc.sync.dma_start(dw_win[:].bitcast(I32), d_words[0].rearrange("p n t -> p (n t)").bitcast(I32))
-        load_tab(3, nc.sync, "xw_win")
+        load_tab(3, nc.sync, "ds_dealt")
 
-        y_bank = [psum.tile([P, S], F32, name="y_bank%d" % t, tag="bank%d" % t) for t in range(PACK)]
-        for t in range(PACK):
+        y_bank = [psum.tile([P, S], F32, name="y_bank%d" % t, tag="bank%d" % t) for t in range(PLANES)]
+        for t in range(PLANES):
             cols = slice(t * P, (t + 1) * P)
             nc.tensor.matmul_mx(
-                y_bank[t][:], lhsT=w_codes[:, cols].bitcast(FP8X4), lhsT_scale=w_plane[:, cols],
-                rhs=x_codes[:].bitcast(FP8X4), rhs_scale=x_plane[:], start=True, stop=True,
+                y_bank[t][:],
+                lhsT=w_codes[:, cols].bitcast(FP8X4),
+                lhsT_scale=w_scale[:, cols],
+                rhs=x_codes[:].bitcast(FP8X4),
+                rhs_scale=x_scale[:],
+                start=True,
+                stop=True,
             )
 
         terms = []
-        for t in range(PACK):
-            y_win = sb.tile([P, WIN], F32, name="y_win%d" % t)
-            g_win = sb.tile([P, WIN], F32, name="g_win%d" % t, align_bytes=64)
-            gate3 = sb.tile([P, S], F32, name="gate3_%d" % t, align_bytes=64)
+        for t in range(PLANES):
+            y_win = sb.tile([P, WINDOW], F32, name="y_win%d" % t, align_bytes=ALIGN)
+            gy_win = sb.tile([P, WINDOW], F32, name="gy_win%d" % t, align_bytes=ALIGN)
             term1 = sb.tile([P, S], F32, name="term1_%d" % t)
             term2 = sb.tile([P, S], F32, name="term2_%d" % t)
             if t == 0:
                 nc.scalar.copy(y_win[:, 0:S], y_bank[t][:])
-                nc.scalar.activation(y_win[:, S:WIN], y_bank[t][:], SIGMOID)
-                nc.vector.tensor_scalar(g_win[:, 0:S], y_win[:, 0:S], gs_t[:, t : t + 1], None, MULT)
+                nc.scalar.activation(y_win[:, S:WINDOW], y_bank[t][:], SIGMOID)
+                nc.vector.tensor_scalar(gy_win[:, 0:S], y_win[:, 0:S], gs_t[:, t : t + 1], None, MULT)
             else:
-                nc.scalar.activation(g_win[:, 0:S], y_bank[t][:], COPY, scale=gs_t[:, t : t + 1])
-                nc.scalar.activation(y_win[:, S:WIN], y_bank[t][:], SIGMOID)
+                nc.scalar.activation(gy_win[:, 0:S], y_bank[t][:], COPY, scale=gs_t[:, t : t + 1])
+                nc.scalar.activation(y_win[:, S:WINDOW], y_bank[t][:], SIGMOID)
                 nc.scalar.copy(y_win[:, 0:S], y_bank[t][:])
-            nc.scalar.activation(gate3[:], y_win[:].indirect(n3_t[:]), SIGMOID)
-            nc.vector.tensor_tensor(term1[:], g_win[:].indirect(n1_t[:]), y_win[:, S:WIN], MULT)
-            pieces = 1 if t < PACK - 1 else 2
+            nc.vector.tensor_tensor(term1[:], gy_win[:].indirect(n1_t[:]), y_win[:, S:WINDOW], MULT)
+            pieces = 2 if t == LAST else 1
             width = S // pieces
             for i in range(pieces):
                 cols = slice(i * width, (i + 1) * width)
-                offsets = n2_t[:, i * width // 16 : (i + 1) * width // 16]
-                nc.vector.tensor_tensor(term2[:, cols], g_win[:].indirect(offsets), gate3[:, cols], MULT)
+                entries = slice(i * width // GROUP, (i + 1) * width // GROUP)
+                gate = sb.tile([P, width], F32, name="gate%d_%d" % (t, i), align_bytes=ALIGN)
+                nc.scalar.activation(gate[:], y_win[:].indirect(n3_t[:, entries]), SIGMOID)
+                nc.vector.tensor_tensor(term2[:, cols], gy_win[:].indirect(n2_t[:, entries]), gate[:], MULT)
             terms.append((term1, term2))
             if t == 0:
-                gather_t4(2, "gate3_0")
+                gather_tab_n4(2, "y_win0")
 
         def add_turned(dst, t, which, b):
             nc.tensor.matmul(
-                dst, lhsT=terms[t][which][:, b * P : (b + 1) * P], rhs=ident[:],
-                start=which == 0, stop=which == 1, is_transpose=True,
+                dst,
+                lhsT=terms[t][which][:, b * P : (b + 1) * P],
+                rhs=ident[:],
+                start=which == 0,
+                stop=which == 1,
+                is_transpose=True,
             )
 
         low = [psum.tile([P, 2, 2, P], F32, name="low%d" % hb, tag="bank%d" % (4 + hb)) for hb in range(2)]
         for t in range(2):
-            for b in range(4):
+            for b in range(BLOCKS):
                 for which in range(2):
                     add_turned(low[b // 2][:, b % 2, t, :], t, which, b)
-        high = [psum.tile([P, 2, P], F32, name="high%d" % b, tag="bank%d" % ((6 + b) % 8)) for b in range(4)]
+        high = [psum.tile([P, 2, P], F32, name="high%d" % b, tag="bank%d" % ((6 + b) % 8)) for b in range(BLOCKS)]
         back = [psum.tile([P, 2, 2, P], F32, name="back%d" % hb, tag="bank%d" % (2 + hb)) for hb in range(2)]
         for which in range(2):
-            for b in range(4):
+            for b in range(BLOCKS):
                 add_turned(high[b][:, 0, :], 2, which, b)
+
         for hb in range(2):
             low_bf = sb.tile([P, 2, P, 2], BF16, name="low_bf%d" % hb)
             nc.scalar.copy(low_bf[:], low[hb][:].rearrange("k b e p -> k b p e"))
@@ -181,8 +211,8 @@ def tile_picked_densewsumkinda_none_p_kernel(
                     back[hb][:, b, 0, :], low_bf[:, b].rearrange("k p e -> k (p e)").bitcast(F32), ident[:]
                 )
         for which in range(2):
-            for b in range(4):
-                add_turned(high[b][:, 1, :], 3, which, b)
+            for b in range(BLOCKS):
+                add_turned(high[b][:, 1, :], LAST, which, b)
         z_bf = []
         for hb in range(2):
             for b in range(2 * hb, 2 * hb + 2):
@@ -191,59 +221,61 @@ def tile_picked_densewsumkinda_none_p_kernel(
                 nc.tensor.transpose(
                     back[hb][:, b % 2, 1, :], high_bf[:].rearrange("k p e -> k (p e)").bitcast(F32), ident[:]
                 )
-            z_bf.append(sb.tile([P, HALF, PACK], BF16, name="z_bf%d" % hb, align_bytes=64))
-            z_words = z_bf[hb][:].rearrange("p k t -> p (k t)").bitcast(F32)
+            z_bf.append(sb.tile([P, HALF, PLANES], BF16, name="z_bf%d" % hb, align_bytes=ALIGN))
+            z_pairs = z_bf[hb][:].rearrange("p k t -> p (k t)").bitcast(F32)
             nc.scalar.copy(
-                z_words.rearrange("p (b k u) -> p b k u", b=2, u=2), back[hb][:].rearrange("p b u k -> p b k u")
+                z_pairs.rearrange("p (b k u) -> p b k u", b=2, u=2), back[hb][:].rearrange("p b u k -> p b k u")
             )
 
-        d_got = sb.tile([P, H], U32, name="d_got", tag="gate3_3", align_bytes=64)
-        nc.vector.tensor_copy(d_got[:], dw_win[:].indirect(k1_t[:]))
-        d_codes = sb.tile([P, H], U32, name="d_codes", align_bytes=64)
-        nc.vector.tensor_copy(
-            d_codes[:].bitcast(I32).rearrange("p (t c i) -> p c t i", t=PACK, i=4),
-            d_got[:].bitcast(I32).rearrange("p (c i t) -> p c t i", t=PACK, i=4),
-        )
-        z_codes = sb.tile([P, S], U32, name="z_codes", align_bytes=64)
-        z_plane = sb.tile([P, S], U8, name="z_plane", align_bytes=64)
+        dw_got = sb.tile([P, H], U32, name="dw_got", tag="gate%d_0" % LAST, align_bytes=ALIGN)
+        nc.vector.tensor_copy(dw_got[:], dw_win[:].indirect(k1_t[:]))
+        d_codes = sb.tile([P, H], U32, name="d_codes", align_bytes=ALIGN)
+        deal_columns(d_codes[:].bitcast(I32), dw_got[:].bitcast(I32))
+        z_codes = sb.tile([P, S], U32, name="z_codes", align_bytes=ALIGN)
+        z_scale = sb.tile([P, S], U8, name="z_scale", align_bytes=ALIGN)
         for hb in range(2):
             half = slice(hb * HALF, (hb + 1) * HALF)
             nc.vector.quantize_mx(
-                z_codes[:, half].bitcast(FP8X4), z_plane[:, half], z_bf[hb][:].rearrange("p k t -> p (k t)")
+                z_codes[:, half].bitcast(FP8X4), z_scale[:, half], z_bf[hb][:].rearrange("p k t -> p (k t)")
             )
-        gather_t4(3, "z_bf1")
+        gather_tab_n4(LAST, "z_bf1")
 
-        h_bank = [psum.tile([P, S], F32, name="h_bank%d" % t, tag="bank%d" % (4 + t)) for t in range(PACK)]
-        for t in range(PACK):
+        h_bank = [psum.tile([P, S], F32, name="h_bank%d" % t, tag="bank%d" % (4 + t)) for t in range(PLANES)]
+        for t in range(PLANES):
             cols = slice(t * P, (t + 1) * P)
             for hb in range(2):
                 half = slice(hb * HALF, (hb + 1) * HALF)
                 nc.tensor.matmul_mx(
                     h_bank[t][:, half],
-                    lhsT=d_codes[:, cols].bitcast(FP8X4), lhsT_scale=d_plane[:, cols],
-                    rhs=z_codes[:, half].bitcast(FP8X4), rhs_scale=z_plane[:, half], start=True, stop=True,
+                    lhsT=d_codes[:, cols].bitcast(FP8X4),
+                    lhsT_scale=d_scale[:, cols],
+                    rhs=z_codes[:, half].bitcast(FP8X4),
+                    rhs_scale=z_scale[:, half],
+                    start=True,
+                    stop=True,
                 )
 
         prods = []
 
         def product(t):
-            h_win = sb.tile([P, WIN], F32, name="h_win%d" % t)
+            h_win = sb.tile([P, WINDOW], F32, name="h_win%d" % t)
             nc.scalar.activation(h_win[:, 0:S], h_bank[t][:], COPY, scale=0.0625)
             prod = sb.tile([P, S], F32, name="prod%d" % t)
-            nc.vector.tensor_tensor(prod[:], h_win[:].indirect(n6_t[:]), t4[t][:], MULT)
+            nc.vector.tensor_tensor(prod[:], h_win[:].indirect(n6_t[:]), tab_n4[t][:], MULT)
             prods.append(prod)
 
         def finish(t, pieces):
             width = S // pieces
             for i in range(pieces):
                 cols = slice(i * width, (i + 1) * width)
+                entries = slice(i * width // GROUP, (i + 1) * width // GROUP)
+                addend = tab_n5_first[:, cols] if t == 0 else tab_win[t][:].indirect(n5_t[:, entries])
                 res = sb.tile([P, width], F32, name="res%d_%d" % (t, i))
-                offsets = n5_t[:, i * width // 16 : (i + 1) * width // 16]
-                nc.vector.tensor_tensor(res[:], tab_win[t][:].indirect(offsets), prods[t][:, cols], ADD)
-                nc.sync.dma_start(out_rows[:, t, cols], res[:])
+                nc.vector.tensor_tensor(res[:], addend, prods[t][:, cols], ADD)
+                nc.sync.dma_start(out_planes[:, t, cols], res[:])
 
         product(0)
-        for t in range(1, PACK):
+        for t in range(1, PLANES):
             product(t)
             finish(t - 1, 1)
-        finish(PACK - 1, 2)
+        finish(LAST, 2)

from contextlib import ExitStack

import concourse.mybir as mybir
from concourse.masks import make_identity

K, T, S, H, G, J = 512, 2048, 512, 512, 2048, 512
FLOPS = 2 * K * H * S + 2 * H * H * S

F32 = mybir.dt.float32
BF16 = mybir.dt.bfloat16
I32 = mybir.dt.int32
U32 = mybir.dt.uint32
U16 = mybir.dt.uint16
U8 = mybir.dt.uint8
FP8X4 = mybir.dt.float8_e4m3fn_x4
MULT = mybir.AluOpType.mult
ADD = mybir.AluOpType.add
COPY = mybir.ActivationFunctionType.Copy
SIGMOID = mybir.ActivationFunctionType.Sigmoid

P = 128
PLANES = 4
LAST = PLANES - 1
GROUP = 16
QUAD = 32
WINDOW = 2 * S
HALF = S // 2
BLOCKS = S // P
ALIGN = 64


def tile_picked_densewsumkinda_none_p_kernel(
    tc, x_words, x_scales, w1, gs, d_words, d_scales, tab, offs, n1, n2, n3, k1, n4, n5, n6, out
):
    nc = tc.nc
    with ExitStack() as ctx:
        lists = ctx.enter_context(tc.tile_pool(name="lists", bufs=1))
        sb = ctx.enter_context(tc.tile_pool(name="sb", bufs=1))
        psum = ctx.enter_context(tc.psum_pool(name="psum", bufs=1))

        def load_list(src, name):
            tile = lists.tile([P, S // GROUP], U16, name=name)
            nc.sync.dma_start(tile[:], src)
            return tile

        tab_planes = tab.rearrange("(p t) j -> p t j", t=PLANES)
        out_planes = out.rearrange("(p t) j -> p t j", t=PLANES)
        tab_win = {}

        def load_tab(t, queue, slot):
            tab_win[t] = sb.tile([P, WINDOW], F32, name="tab_win%d" % t, tag=slot, align_bytes=ALIGN)
            queue.dma_start(tab_win[t][:, 0:J], tab_planes[:, t, :])

        xs_win = sb.tile([P, T], U8, name="xs_win", align_bytes=ALIGN)
        ds_win = sb.tile([P, G], U8, name="ds_win", align_bytes=ALIGN)
        d_scale = sb.tile([P, H], U8, name="d_scale", align_bytes=ALIGN)
        nc.gpsimd.memset(xs_win[:].bitcast(I32), 0)
        warm = sb.tile([P, 8], F32, name="warm")
        nc.vector.memset(warm[:, 0:1], 0.0)
        nc.vector.memset(ds_win[:].bitcast(I32), 0)
        nc.vector.memset(d_scale[:].bitcast(I32), 0)

        ident = sb.tile([P, P], F32, name="ident")
        make_identity(nc, ident[:])

        n4_t = load_list(n4, "n4_t")
        n5_t = load_list(n5, "n5_t")
        load_tab(0, nc.scalar, "tab_win0")
        offs_t = load_list(offs, "offs_t")
        load_tab(1, nc.scalar, "tab_win1")
        xs_rows = x_scales[0].rearrange("(q r) c -> r q c", r=4)
        for r in range(4):
            nc.sync.dma_start(xs_win[r:P:QUAD, :].bitcast(I32), xs_rows[r].bitcast(I32))
        w_rows = w1.rearrange("(p j) c -> p j c", j=PLANES)
        w_raw = [sb.tile([P, PLANES, H // 2], F32, name="w_raw%d" % i, align_bytes=ALIGN) for i in range(2)]
        for i in range(2):
            nc.scalar.dma_start(w_raw[i][:], w_rows[:, :, i * H // 2 : (i + 1) * H // 2])
        xw_win = sb.tile([P, T], U32, name="xw_win", align_bytes=ALIGN)
        nc.scalar.dma_start(xw_win[:].bitcast(I32), x_words[0].rearrange("p n t -> p (n t)").bitcast(I32))
        nc.scalar.activation(warm[:, 4:5], warm[:, 0:1], SIGMOID)
        k1_t = load_list(k1, "k1_t")
        ds_rows = d_scales[0].rearrange("(g e) c -> e g c", e=2)
        for e in range(2):
            nc.sync.dma_start(ds_win[e:P:GROUP, :].bitcast(I32), ds_rows[e].bitcast(I32))
        gs_t = sb.tile([P, PLANES], F32, name="gs_t")
        nc.sync.dma_start(gs_t[:], gs.rearrange("(p t) o -> p (t o)", t=PLANES))
        n1_t = load_list(n1, "n1_t")
        n3_t = load_list(n3, "n3_t")
        n2_t = load_list(n2, "n2_t")
        n6_t = load_list(n6, "n6_t")

        tab_n4 = {}

        def gather_tab_n4(t, slot):
            tab_n4[t] = sb.tile([P, S], F32, name="tab_n4_%d" % t, tag=slot, align_bytes=ALIGN)
            nc.vector.tensor_copy(tab_n4[t][:], tab_win[t][:].indirect(n4_t[:]))

        gather_tab_n4(0, "tab_n4_0")
        gather_tab_n4(1, "tab_n4_1")
        tab_n5_first = sb.tile([P, S], F32, name="tab_n5_first")
        nc.vector.tensor_copy(tab_n5_first[:], tab_win[0][:].indirect(n5_t[:]))
        x_scale = sb.tile([P, S], U8, name="x_scale", align_bytes=ALIGN)
        nc.vector.tensor_copy(x_scale[:], xs_win[:].indirect(offs_t[:]))

        w_bf = sb.tile([P, PLANES, P, PLANES], BF16, name="w_bf", align_bytes=ALIGN)
        for i, planes in ((0, slice(0, 4)), (1, slice(0, 2)), (1, slice(2, 4))):
            nc.scalar.copy(
                w_bf[:, planes, i * P // 2 : (i + 1) * P // 2, :].rearrange("p t m j -> p m t j"),
                w_raw[i][:].rearrange("p j (m t) -> p m t j", t=PLANES)[:, :, planes, :],
            )
        w_codes = sb.tile([P, H], U32, name="w_codes", tag="xs_win", align_bytes=ALIGN)
        w_scale = sb.tile([P, H], U8, name="w_scale", align_bytes=ALIGN)
        x_codes = sb.tile([P, S], U32, name="x_codes", align_bytes=ALIGN)

        def quantise_w(pair):
            cols = slice(pair * H // 2, (pair + 1) * H // 2)
            nc.vector.quantize_mx(
                w_codes[:, cols].bitcast(FP8X4),
                w_scale[:, cols],
                w_bf[:, 2 * pair : 2 * pair + 2].rearrange("p t m j -> p (t m j)"),
            )

        quantise_w(0)
        nc.vector.tensor_copy(x_codes[:], xw_win[:].indirect(offs_t[:]))
        quantise_w(1)
        load_tab(2, nc.sync, "xw_win")

        def deal_columns(dst, src):
            nc.vector.tensor_copy(
                dst.rearrange("p (t c i) -> p c t i", t=PLANES, i=4),
                src.rearrange("p (c i t) -> p c t i", t=PLANES, i=4),
            )

        ds_got = sb.tile([P, H], U8, name="ds_got", tag="w_bf", align_bytes=ALIGN)
        nc.vector.tensor_copy(ds_got[:], ds_win[:].indirect(k1_t[:]))
        ds_dealt = sb.tile([P, H], U8, name="ds_dealt", align_bytes=ALIGN)
        deal_columns(ds_dealt[:], ds_got[:])
        for r in range(4):
            first = GROUP * (r // 2) + r % 2
            nc.sync.dma_start(d_scale[r:P:QUAD, :].bitcast(I32), ds_dealt[first:P:QUAD, :].bitcast(I32))
        dw_win = sb.tile([P, G], U32, name="dw_win", tag="ds_win", align_bytes=ALIGN)
        nc.sync.dma_start(dw_win[:].bitcast(I32), d_words[0].rearrange("p n t -> p (n t)").bitcast(I32))
        load_tab(3, nc.sync, "ds_dealt")

        y_bank = [psum.tile([P, S], F32, name="y_bank%d" % t, tag="bank%d" % t) for t in range(PLANES)]
        for t in range(PLANES):
            cols = slice(t * P, (t + 1) * P)
            nc.tensor.matmul_mx(
                y_bank[t][:],
                lhsT=w_codes[:, cols].bitcast(FP8X4),
                lhsT_scale=w_scale[:, cols],
                rhs=x_codes[:].bitcast(FP8X4),
                rhs_scale=x_scale[:],
                start=True,
                stop=True,
            )

        terms = []
        for t in range(PLANES):
            y_win = sb.tile([P, WINDOW], F32, name="y_win%d" % t, align_bytes=ALIGN)
            gy_win = sb.tile([P, WINDOW], F32, name="gy_win%d" % t, align_bytes=ALIGN)
            term1 = sb.tile([P, S], F32, name="term1_%d" % t)
            term2 = sb.tile([P, S], F32, name="term2_%d" % t)
            if t == 0:
                nc.scalar.copy(y_win[:, 0:S], y_bank[t][:])
                nc.scalar.activation(y_win[:, S:WINDOW], y_bank[t][:], SIGMOID)
                nc.vector.tensor_scalar(gy_win[:, 0:S], y_win[:, 0:S], gs_t[:, t : t + 1], None, MULT)
            else:
                nc.scalar.activation(gy_win[:, 0:S], y_bank[t][:], COPY, scale=gs_t[:, t : t + 1])
                nc.scalar.activation(y_win[:, S:WINDOW], y_bank[t][:], SIGMOID)
                nc.scalar.copy(y_win[:, 0:S], y_bank[t][:])
            nc.vector.tensor_tensor(term1[:], gy_win[:].indirect(n1_t[:]), y_win[:, S:WINDOW], MULT)
            pieces = 2 if t == LAST else 1
            width = S // pieces
            for i in range(pieces):
                cols = slice(i * width, (i + 1) * width)
                entries = slice(i * width // GROUP, (i + 1) * width // GROUP)
                gate = sb.tile([P, width], F32, name="gate%d_%d" % (t, i), align_bytes=ALIGN)
                nc.scalar.activation(gate[:], y_win[:].indirect(n3_t[:, entries]), SIGMOID)
                nc.vector.tensor_tensor(term2[:, cols], gy_win[:].indirect(n2_t[:, entries]), gate[:], MULT)
            terms.append((term1, term2))
            if t == 0:
                gather_tab_n4(2, "y_win0")

        def add_turned(dst, t, which, b):
            nc.tensor.matmul(
                dst,
                lhsT=terms[t][which][:, b * P : (b + 1) * P],
                rhs=ident[:],
                start=which == 0,
                stop=which == 1,
                is_transpose=True,
            )

        low = [psum.tile([P, 2, 2, P], F32, name="low%d" % hb, tag="bank%d" % (4 + hb)) for hb in range(2)]
        for t in range(2):
            for b in range(BLOCKS):
                for which in range(2):
                    add_turned(low[b // 2][:, b % 2, t, :], t, which, b)
        high = [psum.tile([P, 2, P], F32, name="high%d" % b, tag="bank%d" % ((6 + b) % 8)) for b in range(BLOCKS)]
        back = [psum.tile([P, 2, 2, P], F32, name="back%d" % hb, tag="bank%d" % (2 + hb)) for hb in range(2)]
        for which in range(2):
            for b in range(BLOCKS):
                add_turned(high[b][:, 0, :], 2, which, b)

        for hb in range(2):
            low_bf = sb.tile([P, 2, P, 2], BF16, name="low_bf%d" % hb)
            nc.scalar.copy(low_bf[:], low[hb][:].rearrange("k b e p -> k b p e"))
            for b in range(2):
                nc.tensor.transpose(
                    back[hb][:, b, 0, :], low_bf[:, b].rearrange("k p e -> k (p e)").bitcast(F32), ident[:]
                )
        for which in range(2):
            for b in range(BLOCKS):
                add_turned(high[b][:, 1, :], LAST, which, b)
        z_bf = []
        for hb in range(2):
            for b in range(2 * hb, 2 * hb + 2):
                high_bf = sb.tile([P, P, 2], BF16, name="high_bf%d" % b)
                nc.scalar.copy(high_bf[:], high[b][:].rearrange("k e p -> k p e"))
                nc.tensor.transpose(
                    back[hb][:, b % 2, 1, :], high_bf[:].rearrange("k p e -> k (p e)").bitcast(F32), ident[:]
                )
            z_bf.append(sb.tile([P, HALF, PLANES], BF16, name="z_bf%d" % hb, align_bytes=ALIGN))
            z_pairs = z_bf[hb][:].rearrange("p k t -> p (k t)").bitcast(F32)
            nc.scalar.copy(
                z_pairs.rearrange("p (b k u) -> p b k u", b=2, u=2), back[hb][:].rearrange("p b u k -> p b k u")
            )

        dw_got = sb.tile([P, H], U32, name="dw_got", tag="gate%d_0" % LAST, align_bytes=ALIGN)
        nc.vector.tensor_copy(dw_got[:], dw_win[:].indirect(k1_t[:]))
        d_codes = sb.tile([P, H], U32, name="d_codes", align_bytes=ALIGN)
        deal_columns(d_codes[:].bitcast(I32), dw_got[:].bitcast(I32))
        z_codes = sb.tile([P, S], U32, name="z_codes", align_bytes=ALIGN)
        z_scale = sb.tile([P, S], U8, name="z_scale", align_bytes=ALIGN)
        for hb in range(2):
            half = slice(hb * HALF, (hb + 1) * HALF)
            nc.vector.quantize_mx(
                z_codes[:, half].bitcast(FP8X4), z_scale[:, half], z_bf[hb][:].rearrange("p k t -> p (k t)")
            )
        gather_tab_n4(LAST, "z_bf1")

        h_bank = [psum.tile([P, S], F32, name="h_bank%d" % t, tag="bank%d" % (4 + t)) for t in range(PLANES)]
        for t in range(PLANES):
            cols = slice(t * P, (t + 1) * P)
            for hb in range(2):
                half = slice(hb * HALF, (hb + 1) * HALF)
                nc.tensor.matmul_mx(
                    h_bank[t][:, half],
                    lhsT=d_codes[:, cols].bitcast(FP8X4),
                    lhsT_scale=d_scale[:, cols],
                    rhs=z_codes[:, half].bitcast(FP8X4),
                    rhs_scale=z_scale[:, half],
                    start=True,
                    stop=True,
                )

        prods = []

        def product(t):
            h_win = sb.tile([P, WINDOW], F32, name="h_win%d" % t)
            nc.scalar.activation(h_win[:, 0:S], h_bank[t][:], COPY, scale=0.0625)
            prod = sb.tile([P, S], F32, name="prod%d" % t)
            nc.vector.tensor_tensor(prod[:], h_win[:].indirect(n6_t[:]), tab_n4[t][:], MULT)
            prods.append(prod)

        def finish(t, pieces):
            width = S // pieces
            for i in range(pieces):
                cols = slice(i * width, (i + 1) * width)
                entries = slice(i * width // GROUP, (i + 1) * width // GROUP)
                addend = tab_n5_first[:, cols] if t == 0 else tab_win[t][:].indirect(n5_t[:, entries])
                res = sb.tile([P, width], F32, name="res%d_%d" % (t, i))
                nc.vector.tensor_tensor(res[:], addend, prods[t][:, cols], ADD)
                nc.sync.dma_start(out_planes[:, t, cols], res[:])

        product(0)
        for t in range(1, PLANES):
            product(t)
            finish(t - 1, 1)
        finish(LAST, 2)
